import numpy as np
import ml_dtypes


def mxq(x, axis, fmt="e4m3"):
    dtype, down = {"e4m3": (ml_dtypes.float8_e4m3fn, 7), "e5m2": (ml_dtypes.float8_e5m2, 14)}[fmt]
    v = np.moveaxis(np.asarray(x, np.float32).astype(ml_dtypes.bfloat16).astype(np.float64), axis, -1)
    blocks = v.reshape(v.shape[:-1] + (-1, 32))
    amax = np.abs(blocks).max(-1, keepdims=True)
    byte = np.maximum(np.where(amax > 0, np.frexp(amax)[1] - 1 + 127, 0) - down, 1)
    scale = np.exp2(byte - 127.0)
    codes = (blocks / scale).astype(np.float32).astype(dtype).astype(np.float64)
    return np.moveaxis((codes * scale).reshape(v.shape), -1, axis)


WIDE = False


def mx_kscale(k):
    if not WIDE:
        return np.ones(k)
    levels = np.array([10, -10, 5, -5, 0])
    if k % 512:
        return np.exp2(np.random.permutation(np.resize(levels, k // 32))).repeat(32)
    a = np.empty((k // 512, 16))
    for p in range(k // 512):
        a[p, :8] = np.random.permutation(np.resize(levels, 8))
        for g in range(8):
            far = levels[np.abs(levels - a[p, g]) >= 10]
            a[p, g + 8] = far[np.random.randint(len(far))]
    return np.exp2(a.ravel()).repeat(32)


def f64(x):
    return np.asarray(x).astype(np.float64)


def striped(idx):
    return np.tile(idx.reshape(-1, 16).T, (8, 1)).astype(np.uint16)


def unstriped(offs):
    return offs[:16].T.reshape(-1).astype(np.int64)


E2M1 = np.array([0.0, 0.5, 1.0, 1.5, 2.0, 3.0, 4.0, 6.0, -0.0, -0.5, -1.0, -1.5, -2.0, -3.0, -4.0, -6.0])


def pack_weight(w, fmt):
    k, n = w.shape
    w = f64(np.asarray(w, np.float32).astype(ml_dtypes.bfloat16)).reshape(k // 32, 32, n)
    amax = np.abs(w).max(1)
    if fmt == "e4m3":
        byte = np.frexp(amax)[1] - 1 + 127 - 7
    else:
        mant, ex = np.frexp(amax / 6.0)
        byte = np.where(mant > 0.5, ex, ex - 1) + 127
    byte = np.clip(np.where(amax > 0, byte, 1), 1, 254)
    scaled = (w * np.exp2(127.0 - byte)[:, None, :]).reshape(k, n).astype(np.float32)
    by_word = np.ascontiguousarray(scaled.reshape(k // 512, 128, 4, n).transpose(0, 1, 3, 2))
    if fmt == "e4m3":
        words = by_word.astype(ml_dtypes.float8_e4m3fn).view(np.uint8)
    else:
        c = by_word.astype(ml_dtypes.float4_e2m1fn).view(np.uint8) & 0xF
        words = (c[..., 0::2] | (c[..., 1::2] << 4)).reshape(k // 512, 128, 2 * n)
    return np.ascontiguousarray(words), np.ascontiguousarray(byte.astype(np.uint8).reshape(k // 512, 16, n))


def unpack_weight(words, scales, fmt):
    g, _, n = scales.shape
    words = np.ascontiguousarray(words).reshape(g, 128, n, -1)
    if fmt == "e4m3":
        vals = words.view(ml_dtypes.float8_e4m3fn).astype(np.float64)
    else:
        nib = np.empty((g, 128, n, 4), np.uint8)
        nib[..., 0::2] = words & 0xF
        nib[..., 1::2] = words >> 4
        vals = E2M1[nib]
    vals = vals * np.repeat(np.exp2(scales.astype(np.float64) - 127.0), 8, axis=1)[..., None]
    return vals.transpose(0, 1, 3, 2).reshape(g * 512, n)


def planes(y):
    n, m = y.shape
    v = y.astype(np.float32).astype(ml_dtypes.bfloat16).astype(np.float64).reshape(n // 32, 32, m)
    top = np.abs(v).max(1)
    byte = np.clip(np.where(top > 0, np.frexp(top)[1] - 1 + 127 - 7, 1), 1, 254)
    codes = (v * np.exp2(127.0 - byte)[:, None, :]).reshape(n, m).astype(np.float32).astype(ml_dtypes.float8_e4m3fn).view(np.uint8)
    words = codes.reshape(n // 512, 128, 4, m).transpose(0, 1, 3, 2)
    return np.ascontiguousarray(words), np.ascontiguousarray(byte.astype(np.uint8).reshape(n // 512, 16, m))


def silu(v):
    return v / (1.0 + np.exp(-np.maximum(v, -700.0)))


K, T, E, C, D, H, N = 512, 1024, 4, 256, 128, 512, 512


def by_expert(wq, xq, C):
    return np.concatenate([wq[e].T @ xq[:, e * C:(e + 1) * C] for e in range(E)], axis=1)


def setup_inputs():
    n = np.random.standard_normal
    s = mx_kscale(K)
    u = mx_kscale(H)
    first = np.random.permutation(np.repeat(np.arange(E), C))
    slots1 = np.concatenate([np.random.permutation(np.flatnonzero(first == e)) for e in range(E)])
    free = np.ones(T, bool); slots2 = np.empty(E * D, np.int64)
    for e in np.random.permutation(E):
        pick = np.random.permutation(np.flatnonzero(free & (first != e)))[:D]; slots2[e * D:(e + 1) * D] = pick; free[pick] = False
    g1 = np.random.uniform(0.5, 1.0, T); g2 = 1.0 - g1
    x = pack_weight(n((K, T)) * s[:, None], "e4m3")
    w1 = [pack_weight(m, "e4m3") for m in n((E, K, H)) / np.sqrt(K) / s[None, :, None]]
    w3 = [pack_weight(m, "e4m3") for m in n((E, K, H)) / np.sqrt(K) / s[None, :, None] * u]
    w2 = [pack_weight(m, "e4m3") for m in n((E, H, N)) / np.sqrt(H) / u[None, :, None]]
    return {
        "x_words": x[0],
        "x_scales": x[1],
        "w1_words": np.stack([m[0] for m in w1]),
        "w1_scales": np.stack([m[1] for m in w1]),
        "w3_words": np.stack([m[0] for m in w3]),
        "w3_scales": np.stack([m[1] for m in w3]),
        "w2_words": np.stack([m[0] for m in w2]),
        "w2_scales": np.stack([m[1] for m in w2]),
        "gate1": (np.tile(g1[slots1], (128, 1))).astype(np.float32),
        "gate2": (np.tile(g2[slots2], (128, 1))).astype(np.float32),
        "offs": striped(slots1),
        "offs2": striped(slots2),
    }


def reference(x_words, x_scales, w1_words, w1_scales, w3_words, w3_scales, w2_words, w2_scales, gate1, gate2, offs, offs2):
    w1 = np.stack([unpack_weight(w1_words[e], w1_scales[e], "e4m3") for e in range(E)])
    w3 = np.stack([unpack_weight(w3_words[e], w3_scales[e], "e4m3") for e in range(E)])
    w2 = np.stack([unpack_weight(w2_words[e], w2_scales[e], "e4m3") for e in range(E)])
    idx, idx2 = unstriped(offs), unstriped(offs2)
    x = unpack_weight(x_words, x_scales, "e4m3")
    h = silu(by_expert(w1, x[:, idx], C)) * by_expert(w3, x[:, idx], C)
    y = by_expert(w2, mxq(h, 0, "e4m3"), C)
    h = silu(by_expert(w1, x[:, idx2], D)) * by_expert(w3, x[:, idx2], D)
    z = by_expert(w2, mxq(h, 0, "e4m3"), D)
    out = np.zeros((N, T))
    out[:, idx] = f64(gate1[:1]) * y
    out[:, idx2] += f64(gate2[:1]) * z
    out_0 = out
    return (out_0,) + planes(out_0)

@@ -1,0 +1,298 @@
+from contextlib import ExitStack
+
+import concourse.mybir as mybir
+
+K, T, E, C, D, H, N = 512, 1024, 4, 256, 128, 512, 512
+FLOPS = 2 * E * (C + D) * (2 * K * H + H * N)
+
+F32 = mybir.dt.float32
+BF16 = mybir.dt.bfloat16
+I32 = mybir.dt.int32
+U32 = mybir.dt.uint32
+U16 = mybir.dt.uint16
+U8 = mybir.dt.uint8
+FP8X4 = mybir.dt.float8_e4m3fn_x4
+MULT = mybir.AluOpType.mult
+ADD = mybir.AluOpType.add
+SILU = mybir.ActivationFunctionType.Silu
+COPY = mybir.ActivationFunctionType.Copy
+
+P = 128
+PACK = 4
+QUADS = 4
+LIST_COL = 16
+BLOCK = 128
+SLOTS = C + D
+BLOCKS = SLOTS // BLOCK
+CHUNK = 256
+
+
+def tile_moe_ada_glu_silu_kernel(
+    tc, x_words, x_scales, w1_words, w1_scales, w3_words, w3_scales, w2_words, w2_scales,
+    gate1, gate2, offs, offs2, out_0, out_1, out_2,
+):
+    nc = tc.nc
+    with ExitStack() as ctx:
+        keep = ctx.enter_context(tc.tile_pool(name="keep", bufs=1))
+        psum = ctx.enter_context(tc.psum_pool(name="psum", bufs=1))
+
+        def held(shape, dtype, name):
+            return keep.tile(shape, dtype, name=name, align_bytes=64)
+
+        first_list = keep.tile([P, E * C // LIST_COL], U16, name="first_list")
+        second_list = keep.tile([P, E * D // LIST_COL], U16, name="second_list")
+        tok_words = held([P, T], U32, "tok_words")
+        tok_scales = held([P, T], U8, "tok_scales")
+        words_in = {"w1": w1_words, "w3": w3_words, "w2": w2_words}
+        scales_in = {"w1": w1_scales, "w3": w3_scales, "w2": w2_scales}
+        raw_words = {(m, e): held([P, H], U32, f"raw_{m}_{e}") for m in words_in for e in range(E)}
+        dealt_words = {(m, e): held([P, H], U32, f"dealt_{m}_{e}") for m in words_in for e in range(E)}
+        raw_scales = {m: held([P, H], U8, f"raw_scales_{m}") for m in words_in}
+        dealt_scales = {m: held([P, H], U8, f"dealt_scales_{m}") for m in words_in}
+        first_gate = held([P, E * C], F32, "first_gate")
+        second_gate = held([P, E * D], F32, "second_gate")
+        slots = {}
+        hidden = [held([P, SLOTS, PACK], BF16, f"hidden_{e}") for e in range(E)]
+        hid_words = [held([P, SLOTS], U32, f"hid_words_{e}") for e in range(E)]
+        hid_scales = [held([P, SLOTS], U8, f"hid_scales_{e}") for e in range(E)]
+        first_win = [held([P, T], F32, f"first_win_{d}") for d in range(PACK)]
+        second_win = [held([P, T], F32, f"second_win_{d}") for d in range(PACK)]
+        total = held([P, PACK, T], F32, "total")
+        total_bf = held([P, T, PACK], BF16, "total_bf")
+        out_words = held([P, T], U32, "out_words")
+        out_scales = held([P, T], U8, "out_scales")
+
+        nc.vector.memset(tok_scales[:].bitcast(I32), 0)
+        for m in raw_scales:
+            nc.vector.memset(raw_scales[m][:].bitcast(I32), 0)
+        for d in range(PACK):
+            nc.vector.memset(second_win[d][:], 0.0)
+
+        def load_token_scales():
+            for q in range(QUADS):
+                nc.sync.dma_start(
+                    out=tok_scales[32 * q : 32 * q + 4, :].bitcast(I32),
+                    in_=x_scales[0, 4 * q : 4 * q + 4, :].bitcast(I32),
+                )
+
+        def load_weight_scales(m, queue):
+            for q in range(QUADS):
+                queue.dma_start(
+                    out=raw_scales[m][32 * q : 32 * q + 4 * E, :].bitcast(I32),
+                    in_=scales_in[m][:, 0, 4 * q : 4 * q + 4, :].bitcast(I32),
+                )
+
+        def load_weight_words(m, e):
+            nc.sync.dma_start(
+                out=raw_words[m, e][:].bitcast(I32),
+                in_=words_in[m][e, 0].rearrange("p n d -> p (n d)").bitcast(I32),
+            )
+
+        def load_scale_rows(m, q):
+            nc.sync.dma_start(
+                out=raw_scales[m][32 * q : 32 * q + 4 * E, :].bitcast(I32),
+                in_=scales_in[m][:, 0, 4 * q : 4 * q + 4, :].bitcast(I32),
+            )
+
+        nc.sync.dma_start(first_list[:], offs)
+        load_token_scales()
+        load_scale_rows("w1", 0)
+        load_scale_rows("w1", 1)
+        nc.sync.dma_start(
+            out=tok_words[:].bitcast(I32), in_=x_words[0].rearrange("p t d -> p (t d)").bitcast(I32)
+        )
+        load_weight_words("w1", 0)
+        load_scale_rows("w1", 2)
+        load_scale_rows("w1", 3)
+        load_weight_words("w3", 0)
+        load_weight_scales("w3", nc.sync)
+        load_weight_words("w2", 0)
+        load_weight_scales("w2", nc.sync)
+        nc.sync.dma_start(out=first_gate[:, 0:C], in_=gate1[:, 0:C])
+        nc.sync.dma_start(second_list[:], offs2)
+        load_weight_words("w1", 1)
+        load_weight_words("w3", 1)
+        nc.sync.dma_start(out=second_gate[:], in_=gate2)
+        load_weight_words("w2", 1)
+        nc.sync.dma_start(out=first_gate[:, C:], in_=gate1[:, C:])
+        for e in range(2, E):
+            for m in words_in:
+                load_weight_words(m, e)
+
+        def second_offsets(e):
+            return second_list[:, e * D // LIST_COL : (e + 1) * D // LIST_COL]
+
+        def block_offsets(e, b):
+            if b < C // BLOCK:
+                start = (e * C + b * BLOCK) // LIST_COL
+                return first_list[:, start : start + BLOCK // LIST_COL]
+            return second_offsets(e)
+
+        def gather(e, b):
+            words = keep.tile([P, BLOCK], U32, name="slot_words", bufs=2, align_bytes=64)
+            scales = keep.tile([P, BLOCK], U8, name="slot_scales", bufs=2, align_bytes=64)
+            nc.vector.tensor_copy(words[:], tok_words[:].indirect(block_offsets(e, b)))
+            nc.vector.tensor_copy(scales[:], tok_scales[:].indirect(block_offsets(e, b)))
+            slots[e, b] = (words[:], scales[:])
+
+        def deal_words(m, e):
+            dst = dealt_words[m, e][:].rearrange("p (d r) -> p r d", d=PACK)
+            src = raw_words[m, e][:].rearrange("p (r d) -> p r d", d=PACK)
+            if e == 0 or (e == 1 and m != "w2"):
+                nc.scalar.copy(out=dst, in_=src)
+            else:
+                nc.vector.tensor_copy(out=dst.bitcast(I32), in_=src.bitcast(I32))
+
+        def deal_scales(m):
+            engine = nc.gpsimd if m == "w2" else nc.vector
+            engine.tensor_copy(
+                out=dealt_scales[m][:].rearrange("p (d r) -> p r d", d=PACK),
+                in_=raw_scales[m][:].rearrange("p (r d) -> p r d", d=PACK),
+            )
+
+        def product(out, m, e, d, words, scales):
+            cols = slice(d * P, (d + 1) * P)
+            nc.tensor.matmul_mx(
+                out=out,
+                lhsT=dealt_words[m, e][:, cols].bitcast(FP8X4),
+                lhsT_scale=dealt_scales[m][4 * e : P, cols],
+                rhs=words.bitcast(FP8X4),
+                rhs_scale=scales,
+                start=True,
+                stop=True,
+            )
+
+        def first_layer(e, b):
+            cols = slice(b * BLOCK, (b + 1) * BLOCK)
+            pre = psum.tile([P, PACK, BLOCK], F32, name="pre", bufs=2)
+            lin = psum.tile([P, PACK, BLOCK], F32, name="lin", bufs=3)
+            for bank, m in ((pre, "w1"), (lin, "w3")):
+                for d in range(PACK):
+                    product(bank[:, d, :], m, e, d, *slots[e, b])
+            act = keep.tile([P, BLOCK, PACK], F32, name="act", bufs=2)
+            nc.scalar.activation(out=act[:], in_=pre[:].rearrange("p d s -> p s d"), func=SILU)
+            nc.vector.tensor_tensor(
+                out=hidden[e][:, cols, :], in0=lin[:].rearrange("p d s -> p s d"), in1=act[:], op=MULT
+            )
+
+        def quantise_hidden(e, b):
+            cols = slice(b * BLOCK, (b + 1) * BLOCK)
+            nc.vector.quantize_mx(
+                out=hid_words[e][:, cols].bitcast(FP8X4),
+                scales=hid_scales[e][:, cols],
+                in_=hidden[e][:, cols, :].rearrange("p s d -> p (s d)"),
+            )
+
+        results = {}
+
+        def second_layer(e, b):
+            cols = slice(b * BLOCK, (b + 1) * BLOCK)
+            res = psum.tile([P, PACK, BLOCK], F32, name="res", bufs=3)
+            for d in range(PACK):
+                product(res[:, d, :], "w2", e, d, hid_words[e][:, cols], hid_scales[e][:, cols])
+            if b < C // BLOCK:
+                gate = first_gate[:, e * C + b * BLOCK : e * C + (b + 1) * BLOCK]
+            else:
+                gate = second_gate[:, e * D : (e + 1) * D]
+            gated = keep.tile([P, PACK, BLOCK], F32, name="gated", bufs=12)
+            nc.vector.tensor_tensor(
+                out=gated[:], in0=res[:], in1=gate.unsqueeze(1).broadcast_to([P, PACK, BLOCK]), op=MULT
+            )
+            results[e, b] = gated
+
+        def scatter(e, b, d):
+            windows = first_win if b < C // BLOCK else second_win
+            window = windows[d][:].indirect(block_offsets(e, b))
+            if d == 3:
+                nc.vector.tensor_copy(window, results[e, b][:, d, :])
+            else:
+                nc.scalar.activation(out=window, in_=results[e, b][:, d, :], func=COPY)
+
+        def finish(d, cols):
+            engine = nc.vector
+            engine.tensor_tensor(
+                out=total[:, d, cols], in0=first_win[d][:, cols], in1=second_win[d][:, cols], op=ADD
+            )
+
+        out_rows = out_0.rearrange("(p d) t -> p d t", d=PACK)
+
+        blocks = [(e, b) for e in range(E) for b in range(BLOCKS)]
+        count = len(blocks)
+        held_back = count - BLOCKS
+        gather(*blocks[0])
+        deal_words("w1", 0)
+        deal_scales("w1")
+        deal_words("w3", 0)
+        deal_scales("w3")
+        gather(*blocks[1])
+        first_layer(*blocks[0])
+        deal_words("w2", 0)
+        deal_scales("w2")
+        for step in range(count + 1):
+            if step + 2 < count:
+                gather(*blocks[step + 2])
+            if step < count:
+                quantise_hidden(*blocks[step])
+            if step + 1 < count:
+                first_layer(*blocks[step + 1])
+            if step < held_back:
+                second_layer(*blocks[step])
+            nxt = step // BLOCKS + 1
+            if nxt < E:
+                if step % BLOCKS == 0:
+                    deal_words("w1", nxt)
+                    deal_words("w3", nxt)
+                if step % BLOCKS == 1:
+                    deal_words("w2", nxt)
+            if 0 <= step - 1 < held_back:
+                for d in range(PACK):
+                    scatter(*blocks[step - 1], d)
+        order = [0, 3, 1, 2]
+        e = E - 1
+        for d in order:
+            res = psum.tile([P, SLOTS], F32, name="res", bufs=3)
+            gated = keep.tile([P, SLOTS], F32, name=f"gated_last_{d}")
+            for cols, gate in ((slice(0, C), first_gate[:, e * C :]), (slice(C, SLOTS), second_gate[:, e * D :])):
+                product(res[:, cols], "w2", e, d, hid_words[e][:, cols], hid_scales[e][:, cols])
+            for cols, gate in ((slice(0, C), first_gate[:, e * C :]), (slice(C, SLOTS), second_gate[:, e * D :])):
+                nc.vector.tensor_tensor(out=gated[:, cols], in0=res[:, cols], in1=gate, op=MULT)
+            results[d] = gated
+        for d in order:
+            first_window = first_win[d][:].indirect(first_list[:, e * C // LIST_COL :])
+            second_window = second_win[d][:].indirect(second_offsets(e))
+            for part, (window, cols) in enumerate(((first_window, slice(0, C)), (second_window, slice(C, SLOTS)))):
+                if d == 3:
+                    nc.vector.tensor_copy(window, results[d][:, cols])
+                else:
+                    nc.scalar.activation(out=window, in_=results[d][:, cols], func=COPY)
+            if d != order[-1]:
+                finish(d, slice(0, T))
+                nc.sync.dma_start(out=out_rows[:, d, :], in_=total[:, d, :])
+
+        last = order[-1]
+        chunks = [slice(c * CHUNK, (c + 1) * CHUNK) for c in range(T // CHUNK)]
+        for cols in chunks:
+            finish(last, cols)
+        nc.sync.dma_start(out=out_rows[:, last, :], in_=total[:, last, :])
+        words_out = out_1[0].rearrange("p t d -> p (t d)").bitcast(I32)
+        for c, cols in enumerate(chunks):
+            dst = total_bf[:, cols, :].rearrange("p (c i) d -> p c d i", i=4)
+            src = total[:, :, cols].rearrange("p d (c i) -> p c d i", i=4)
+            if c % 2 == 0:
+                nc.scalar.copy(out=dst, in_=src)
+            else:
+                nc.vector.tensor_copy(out=dst, in_=src)
+        for c in (1, 0, 3, 2):
+            cols = chunks[c]
+            nc.vector.quantize_mx(
+                out=out_words[:, cols].bitcast(FP8X4),
+                scales=out_scales[:, cols],
+                in_=total_bf[:, cols, :].rearrange("p t d -> p (t d)"),
+            )
+            nc.sync.dma_start(out=words_out[:, cols], in_=out_words[:, cols].bitcast(I32))
+        for q in range(QUADS):
+            queue = nc.sync if q % 2 == 0 else nc.scalar
+            queue.dma_start(
+                out=out_2[0, 4 * q : 4 * q + 4, :].bitcast(I32),
+                in_=out_scales[32 * q : 32 * q + 4, :].bitcast(I32),
+            )

@@ -49,8 +49,7 @@ def tile_moe_ada_glu_silu_kernel(
         dealt_words = {(m, e): held([P, H], U32, f"dealt_{m}_{e}") for m in words_in for e in range(E)}
         raw_scales = {m: held([P, H], U8, f"raw_scales_{m}") for m in words_in}
         dealt_scales = {m: held([P, H], U8, f"dealt_scales_{m}") for m in words_in}
-        first_gate = held([P, E * C], F32, "first_gate")
-        second_gate = held([P, E * D], F32, "second_gate")
+        gates = [held([P, SLOTS], F32, f"gates_{e}") for e in range(E)]
         slots = {}
         hidden = [held([P, SLOTS, PACK], BF16, f"hidden_{e}") for e in range(E)]
         hid_words = [held([P, SLOTS], U32, f"hid_words_{e}") for e in range(E)]
@@ -62,11 +61,12 @@ def tile_moe_ada_glu_silu_kernel(
         out_words = held([P, T], U32, "out_words")
         out_scales = held([P, T], U8, "out_scales")
 
-        nc.vector.memset(tok_scales[:].bitcast(I32), 0)
+        nc.gpsimd.memset(tok_scales[:].bitcast(I32), 0)
         for m in raw_scales:
-            nc.vector.memset(raw_scales[m][:].bitcast(I32), 0)
+            nc.gpsimd.memset(raw_scales[m][:].bitcast(I32), 0)
         for d in range(PACK):
-            nc.vector.memset(second_win[d][:], 0.0)
+            engine = nc.vector if d < 2 else nc.gpsimd
+            engine.memset(second_win[d][:], 0.0)
 
         def load_token_scales():
             for q in range(QUADS):
@@ -94,30 +94,47 @@ def tile_moe_ada_glu_silu_kernel(
                 in_=scales_in[m][:, 0, 4 * q : 4 * q + 4, :].bitcast(I32),
             )
 
+        def load_token_words():
+            nc.sync.dma_start(
+                out=tok_words[:].bitcast(I32), in_=x_words[0].rearrange("p t d -> p (t d)").bitcast(I32)
+            )
+
+        def load_gates(e, part):
+            if part == 0:
+                nc.sync.dma_start(out=gates[e][:, 0:C], in_=gate1[:, e * C : (e + 1) * C])
+            else:
+                nc.sync.dma_start(out=gates[e][:, C:SLOTS], in_=gate2[:, e * D : (e + 1) * D])
+
         nc.sync.dma_start(first_list[:], offs)
         load_token_scales()
         load_scale_rows("w1", 0)
         load_scale_rows("w1", 1)
-        nc.sync.dma_start(
-            out=tok_words[:].bitcast(I32), in_=x_words[0].rearrange("p t d -> p (t d)").bitcast(I32)
-        )
+        load_token_words()
         load_weight_words("w1", 0)
         load_scale_rows("w1", 2)
         load_scale_rows("w1", 3)
         load_weight_words("w3", 0)
         load_weight_scales("w3", nc.sync)
-        load_weight_words("w2", 0)
-        load_weight_scales("w2", nc.sync)
-        nc.sync.dma_start(out=first_gate[:, 0:C], in_=gate1[:, 0:C])
         nc.sync.dma_start(second_list[:], offs2)
+        load_weight_scales("w2", nc.sync)
+        load_weight_words("w2", 0)
+        load_gates(0, 0)
         load_weight_words("w1", 1)
         load_weight_words("w3", 1)
-        nc.sync.dma_start(out=second_gate[:], in_=gate2)
+        load_gates(0, 1)
         load_weight_words("w2", 1)
-        nc.sync.dma_start(out=first_gate[:, C:], in_=gate1[:, C:])
-        for e in range(2, E):
-            for m in words_in:
-                load_weight_words(m, e)
+        load_gates(1, 0)
+        load_gates(1, 1)
+        load_weight_words("w1", 2)
+        load_weight_words("w3", 2)
+        load_weight_words("w2", 2)
+        load_gates(2, 0)
+        load_gates(2, 1)
+        load_weight_words("w1", 3)
+        load_weight_words("w3", 3)
+        load_weight_words("w2", 3)
+        load_gates(3, 0)
+        load_gates(3, 1)
 
         def second_offsets(e):
             return second_list[:, e * D // LIST_COL : (e + 1) * D // LIST_COL]
@@ -129,23 +146,28 @@ def tile_moe_ada_glu_silu_kernel(
             return second_offsets(e)
 
         def gather(e, b):
-            words = keep.tile([P, BLOCK], U32, name="slot_words", bufs=2, align_bytes=64)
-            scales = keep.tile([P, BLOCK], U8, name="slot_scales", bufs=2, align_bytes=64)
-            nc.vector.tensor_copy(words[:], tok_words[:].indirect(block_offsets(e, b)))
-            nc.vector.tensor_copy(scales[:], tok_scales[:].indirect(block_offsets(e, b)))
-            slots[e, b] = (words[:], scales[:])
+            if b == 1:
+                return
+            width = C if b == 0 else D
+            offsets = first_list[:, e * C // LIST_COL : (e + 1) * C // LIST_COL] if b == 0 else second_offsets(e)
+            words = keep.tile([P, width], U32, name=f"slot_words_{width}", bufs=1, align_bytes=64)
+            scales = keep.tile([P, width], U8, name=f"slot_scales_{width}", bufs=1, align_bytes=64)
+            nc.vector.tensor_copy(scales[:], tok_scales[:].indirect(offsets))
+            nc.vector.tensor_copy(words[:], tok_words[:].indirect(offsets))
+            for j in range(width // BLOCK):
+                part = slice(j * BLOCK, (j + 1) * BLOCK)
+                slots[e, b + j] = (words[:, part], scales[:, part])
 
         def deal_words(m, e):
             dst = dealt_words[m, e][:].rearrange("p (d r) -> p r d", d=PACK)
             src = raw_words[m, e][:].rearrange("p (r d) -> p r d", d=PACK)
-            if e == 0 or (e == 1 and m != "w2"):
+            if (e == 0 and m == "w2") or (e == 1 and m != "w2"):
                 nc.scalar.copy(out=dst, in_=src)
             else:
                 nc.vector.tensor_copy(out=dst.bitcast(I32), in_=src.bitcast(I32))
 
         def deal_scales(m):
-            engine = nc.gpsimd if m == "w2" else nc.vector
-            engine.tensor_copy(
+            nc.vector.tensor_copy(
                 out=dealt_scales[m][:].rearrange("p (d r) -> p r d", d=PACK),
                 in_=raw_scales[m][:].rearrange("p (r d) -> p r d", d=PACK),
             )
@@ -190,10 +212,7 @@ def tile_moe_ada_glu_silu_kernel(
             res = psum.tile([P, PACK, BLOCK], F32, name="res", bufs=3)
             for d in range(PACK):
                 product(res[:, d, :], "w2", e, d, hid_words[e][:, cols], hid_scales[e][:, cols])
-            if b < C // BLOCK:
-                gate = first_gate[:, e * C + b * BLOCK : e * C + (b + 1) * BLOCK]
-            else:
-                gate = second_gate[:, e * D : (e + 1) * D]
+            gate = gates[e][:, cols]
             gated = keep.tile([P, PACK, BLOCK], F32, name="gated", bufs=12)
             nc.vector.tensor_tensor(
                 out=gated[:], in0=res[:], in1=gate.unsqueeze(1).broadcast_to([P, PACK, BLOCK]), op=MULT
@@ -203,7 +222,7 @@ def tile_moe_ada_glu_silu_kernel(
         def scatter(e, b, d):
             windows = first_win if b < C // BLOCK else second_win
             window = windows[d][:].indirect(block_offsets(e, b))
-            if d == 3:
+            if d == 3 or (d == 2 and b == 2 and e == 0):
                 nc.vector.tensor_copy(window, results[e, b][:, d, :])
             else:
                 nc.scalar.activation(out=window, in_=results[e, b][:, d, :], func=COPY)
@@ -249,15 +268,14 @@ def tile_moe_ada_glu_silu_kernel(
                     scatter(*blocks[step - 1], d)
         order = [0, 3, 1, 2]
         e = E - 1
-        for d in order:
-            res = psum.tile([P, SLOTS], F32, name="res", bufs=3)
+        for j, d in enumerate(order):
+            res = psum.tile([P, SLOTS], F32, name="res" if j < 3 else "lin", bufs=3)
             gated = keep.tile([P, SLOTS], F32, name=f"gated_last_{d}")
-            for cols, gate in ((slice(0, C), first_gate[:, e * C :]), (slice(C, SLOTS), second_gate[:, e * D :])):
+            for cols in (slice(0, C), slice(C, SLOTS)):
                 product(res[:, cols], "w2", e, d, hid_words[e][:, cols], hid_scales[e][:, cols])
-            for cols, gate in ((slice(0, C), first_gate[:, e * C :]), (slice(C, SLOTS), second_gate[:, e * D :])):
-                nc.vector.tensor_tensor(out=gated[:, cols], in0=res[:, cols], in1=gate, op=MULT)
+            nc.vector.tensor_tensor(out=gated[:], in0=res[:], in1=gates[e][:], op=MULT)
             results[d] = gated
-        for d in order:
+        def scatter_last(d):
             first_window = first_win[d][:].indirect(first_list[:, e * C // LIST_COL :])
             second_window = second_win[d][:].indirect(second_offsets(e))
             for part, (window, cols) in enumerate(((first_window, slice(0, C)), (second_window, slice(C, SLOTS)))):
@@ -265,9 +283,12 @@ def tile_moe_ada_glu_silu_kernel(
                     nc.vector.tensor_copy(window, results[d][:, cols])
                 else:
                     nc.scalar.activation(out=window, in_=results[d][:, cols], func=COPY)
-            if d != order[-1]:
-                finish(d, slice(0, T))
-                nc.sync.dma_start(out=out_rows[:, d, :], in_=total[:, d, :])
+
+        for d in order:
+            scatter_last(d)
+        for d in [3, 0, 1]:
+            finish(d, slice(0, T))
+            nc.sync.dma_start(out=out_rows[:, d, :], in_=total[:, d, :])
 
         last = order[-1]
         chunks = [slice(c * CHUNK, (c + 1) * CHUNK) for c in range(T // CHUNK)]

@@ -168,8 +168,8 @@ def tile_moe_ada_glu_silu_kernel(
 
         def deal_scales(m):
             nc.vector.tensor_copy(
-                out=dealt_scales[m][:].rearrange("p (d r) -> p r d", d=PACK),
-                in_=raw_scales[m][:].rearrange("p (r d) -> p r d", d=PACK),
+                out=dealt_scales[m][:].rearrange("p (d r) -> p d r", d=PACK),
+                in_=raw_scales[m][:].rearrange("p (r d) -> p d r", d=PACK),
             )
 
         def product(out, m, e, d, words, scales):

@@ -24,6 +24,8 @@ LIST_COL = 16
 BLOCK = 128
 SLOTS = C + D
 BLOCKS = SLOTS // BLOCK
+FIRST_BLOCKS = C // BLOCK
+VECTOR_ROW_SET = 3
 CHUNK = 256
 
 
@@ -50,7 +52,6 @@ def tile_moe_ada_glu_silu_kernel(
         raw_scales = {m: held([P, H], U8, f"raw_scales_{m}") for m in words_in}
         dealt_scales = {m: held([P, H], U8, f"dealt_scales_{m}") for m in words_in}
         gates = [held([P, SLOTS], F32, f"gates_{e}") for e in range(E)]
-        slots = {}
         hidden = [held([P, SLOTS, PACK], BF16, f"hidden_{e}") for e in range(E)]
         hid_words = [held([P, SLOTS], U32, f"hid_words_{e}") for e in range(E)]
         hid_scales = [held([P, SLOTS], U8, f"hid_scales_{e}") for e in range(E)]
@@ -65,19 +66,12 @@ def tile_moe_ada_glu_silu_kernel(
         for m in raw_scales:
             nc.gpsimd.memset(raw_scales[m][:].bitcast(I32), 0)
         for d in range(PACK):
-            engine = nc.vector if d < 2 else nc.gpsimd
+            engine = nc.vector if d < PACK // 2 else nc.gpsimd
             engine.memset(second_win[d][:], 0.0)
 
-        def load_token_scales():
-            for q in range(QUADS):
+        def load_weight_scales(m, quads):
+            for q in quads:
                 nc.sync.dma_start(
-                    out=tok_scales[32 * q : 32 * q + 4, :].bitcast(I32),
-                    in_=x_scales[0, 4 * q : 4 * q + 4, :].bitcast(I32),
-                )
-
-        def load_weight_scales(m, queue):
-            for q in range(QUADS):
-                queue.dma_start(
                     out=raw_scales[m][32 * q : 32 * q + 4 * E, :].bitcast(I32),
                     in_=scales_in[m][:, 0, 4 * q : 4 * q + 4, :].bitcast(I32),
                 )
@@ -88,80 +82,67 @@ def tile_moe_ada_glu_silu_kernel(
                 in_=words_in[m][e, 0].rearrange("p n d -> p (n d)").bitcast(I32),
             )
 
-        def load_scale_rows(m, q):
-            nc.sync.dma_start(
-                out=raw_scales[m][32 * q : 32 * q + 4 * E, :].bitcast(I32),
-                in_=scales_in[m][:, 0, 4 * q : 4 * q + 4, :].bitcast(I32),
-            )
+        def load_first_gate(e):
+            nc.sync.dma_start(out=gates[e][:, 0:C], in_=gate1[:, e * C : (e + 1) * C])
 
-        def load_token_words():
-            nc.sync.dma_start(
-                out=tok_words[:].bitcast(I32), in_=x_words[0].rearrange("p t d -> p (t d)").bitcast(I32)
-            )
-
-        def load_gates(e, part):
-            if part == 0:
-                nc.sync.dma_start(out=gates[e][:, 0:C], in_=gate1[:, e * C : (e + 1) * C])
-            else:
-                nc.sync.dma_start(out=gates[e][:, C:SLOTS], in_=gate2[:, e * D : (e + 1) * D])
+        def load_second_gate(e):
+            nc.sync.dma_start(out=gates[e][:, C:SLOTS], in_=gate2[:, e * D : (e + 1) * D])
 
         nc.sync.dma_start(first_list[:], offs)
-        load_token_scales()
-        load_scale_rows("w1", 0)
-        load_scale_rows("w1", 1)
-        load_token_words()
+        for q in range(QUADS):
+            nc.sync.dma_start(
+                out=tok_scales[32 * q : 32 * q + 4, :].bitcast(I32),
+                in_=x_scales[0, 4 * q : 4 * q + 4, :].bitcast(I32),
+            )
+        load_weight_scales("w1", range(0, QUADS // 2))
+        nc.sync.dma_start(
+            out=tok_words[:].bitcast(I32), in_=x_words[0].rearrange("p t d -> p (t d)").bitcast(I32)
+        )
         load_weight_words("w1", 0)
-        load_scale_rows("w1", 2)
-        load_scale_rows("w1", 3)
+        load_weight_scales("w1", range(QUADS // 2, QUADS))
         load_weight_words("w3", 0)
-        load_weight_scales("w3", nc.sync)
+        load_weight_scales("w3", range(QUADS))
         nc.sync.dma_start(second_list[:], offs2)
-        load_weight_scales("w2", nc.sync)
-        load_weight_words("w2", 0)
-        load_gates(0, 0)
-        load_weight_words("w1", 1)
-        load_weight_words("w3", 1)
-        load_gates(0, 1)
-        load_weight_words("w2", 1)
-        load_gates(1, 0)
-        load_gates(1, 1)
-        load_weight_words("w1", 2)
-        load_weight_words("w3", 2)
-        load_weight_words("w2", 2)
-        load_gates(2, 0)
-        load_gates(2, 1)
-        load_weight_words("w1", 3)
-        load_weight_words("w3", 3)
-        load_weight_words("w2", 3)
-        load_gates(3, 0)
-        load_gates(3, 1)
+        load_weight_scales("w2", range(QUADS))
+        for e in range(E - 1):
+            load_weight_words("w1", e + 1)
+            load_weight_words("w2", e)
+            load_first_gate(e)
+            load_weight_words("w3", e + 1)
+            load_second_gate(e)
+        load_weight_words("w2", E - 1)
+        load_first_gate(E - 1)
+        load_second_gate(E - 1)
+
+        def first_offsets(start, width):
+            return first_list[:, start // LIST_COL : (start + width) // LIST_COL]
 
         def second_offsets(e):
             return second_list[:, e * D // LIST_COL : (e + 1) * D // LIST_COL]
 
-        def block_offsets(e, b):
-            if b < C // BLOCK:
-                start = (e * C + b * BLOCK) // LIST_COL
-                return first_list[:, start : start + BLOCK // LIST_COL]
-            return second_offsets(e)
+        slots = {}
 
-        def gather(e, b):
-            if b == 1:
-                return
-            width = C if b == 0 else D
-            offsets = first_list[:, e * C // LIST_COL : (e + 1) * C // LIST_COL] if b == 0 else second_offsets(e)
-            words = keep.tile([P, width], U32, name=f"slot_words_{width}", bufs=1, align_bytes=64)
-            scales = keep.tile([P, width], U8, name=f"slot_scales_{width}", bufs=1, align_bytes=64)
+        def gather(name, offsets, e, first_block, width):
+            words = held([P, width], U32, f"{name}_words")
+            scales = held([P, width], U8, f"{name}_scales")
             nc.vector.tensor_copy(scales[:], tok_scales[:].indirect(offsets))
             nc.vector.tensor_copy(words[:], tok_words[:].indirect(offsets))
             for j in range(width // BLOCK):
                 part = slice(j * BLOCK, (j + 1) * BLOCK)
-                slots[e, b + j] = (words[:, part], scales[:, part])
+                slots[e, first_block + j] = (words[:, part], scales[:, part])
+
+        def gather_for(e, b):
+            if b == 0:
+                gather("first_slot", first_offsets(e * C, C), e, b, C)
+            if b == FIRST_BLOCKS:
+                gather("second_slot", second_offsets(e), e, b, D)
+
+        dealt_by_scalar = [("w2", 0), ("w1", 1), ("w3", 1)]
 
         def deal_words(m, e):
             dst = dealt_words[m, e][:].rearrange("p (d r) -> p r d", d=PACK)
             src = raw_words[m, e][:].rearrange("p (r d) -> p r d", d=PACK)
-            if (e == 0 and m == "w2") or (e == 1 and m != "w2"):
+            if (m, e) in dealt_by_scalar:
                 nc.scalar.copy(out=dst, in_=src)
             else:
                 nc.vector.tensor_copy(out=dst.bitcast(I32), in_=src.bitcast(I32))
@@ -184,8 +165,10 @@ def tile_moe_ada_glu_silu_kernel(
                 stop=True,
             )
 
+        def block_cols(b):
+            return slice(b * BLOCK, (b + 1) * BLOCK)
+
         def first_layer(e, b):
-            cols = slice(b * BLOCK, (b + 1) * BLOCK)
             pre = psum.tile([P, PACK, BLOCK], F32, name="pre", bufs=2)
             lin = psum.tile([P, PACK, BLOCK], F32, name="lin", bufs=3)
             for bank, m in ((pre, "w1"), (lin, "w3")):
@@ -194,123 +177,116 @@ def tile_moe_ada_glu_silu_kernel(
             act = keep.tile([P, BLOCK, PACK], F32, name="act", bufs=2)
             nc.scalar.activation(out=act[:], in_=pre[:].rearrange("p d s -> p s d"), func=SILU)
             nc.vector.tensor_tensor(
-                out=hidden[e][:, cols, :], in0=lin[:].rearrange("p d s -> p s d"), in1=act[:], op=MULT
+                out=hidden[e][:, block_cols(b), :], in0=lin[:].rearrange("p d s -> p s d"), in1=act[:], op=MULT
             )
 
         def quantise_hidden(e, b):
-            cols = slice(b * BLOCK, (b + 1) * BLOCK)
+            cols = block_cols(b)
             nc.vector.quantize_mx(
                 out=hid_words[e][:, cols].bitcast(FP8X4),
                 scales=hid_scales[e][:, cols],
                 in_=hidden[e][:, cols, :].rearrange("p s d -> p (s d)"),
             )
 
-        results = {}
+        gated_blocks = {}
 
         def second_layer(e, b):
-            cols = slice(b * BLOCK, (b + 1) * BLOCK)
+            cols = block_cols(b)
             res = psum.tile([P, PACK, BLOCK], F32, name="res", bufs=3)
             for d in range(PACK):
                 product(res[:, d, :], "w2", e, d, hid_words[e][:, cols], hid_scales[e][:, cols])
-            gate = gates[e][:, cols]
-            gated = keep.tile([P, PACK, BLOCK], F32, name="gated", bufs=12)
-            nc.vector.tensor_tensor(
-                out=gated[:], in0=res[:], in1=gate.unsqueeze(1).broadcast_to([P, PACK, BLOCK]), op=MULT
-            )
-            results[e, b] = gated
+            gated = keep.tile([P, PACK, BLOCK], F32, name=f"gated_{e}_{b}")
+            gate = gates[e][:, cols].unsqueeze(1).broadcast_to([P, PACK, BLOCK])
+            nc.vector.tensor_tensor(out=gated[:], in0=res[:], in1=gate, op=MULT)
+            gated_blocks[e, b] = gated
 
-        def scatter(e, b, d):
-            windows = first_win if b < C // BLOCK else second_win
-            window = windows[d][:].indirect(block_offsets(e, b))
-            if d == 3 or (d == 2 and b == 2 and e == 0):
-                nc.vector.tensor_copy(window, results[e, b][:, d, :])
+        def scatter(d, window, offsets, values):
+            if d == VECTOR_ROW_SET:
+                nc.vector.tensor_copy(window[:].indirect(offsets), values)
             else:
-                nc.scalar.activation(out=window, in_=results[e, b][:, d, :], func=COPY)
+                nc.scalar.activation(out=window[:].indirect(offsets), in_=values, func=COPY)
 
-        def finish(d, cols):
-            engine = nc.vector
-            engine.tensor_tensor(
+        def scatter_block(e, b):
+            for d in range(PACK):
+                values = gated_blocks[e, b][:, d, :]
+                if b < FIRST_BLOCKS:
+                    scatter(d, first_win[d], first_offsets(e * C + b * BLOCK, BLOCK), values)
+                else:
+                    scatter(d, second_win[d], second_offsets(e), values)
+
+        def add_choices(d, cols):
+            nc.vector.tensor_tensor(
                 out=total[:, d, cols], in0=first_win[d][:, cols], in1=second_win[d][:, cols], op=ADD
             )
 
         out_rows = out_0.rearrange("(p d) t -> p d t", d=PACK)
 
         blocks = [(e, b) for e in range(E) for b in range(BLOCKS)]
-        count = len(blocks)
-        held_back = count - BLOCKS
-        gather(*blocks[0])
-        deal_words("w1", 0)
-        deal_scales("w1")
-        deal_words("w3", 0)
-        deal_scales("w3")
-        gather(*blocks[1])
+        before_last_expert = len(blocks) - BLOCKS
+        gather_for(*blocks[0])
+        for m in ("w1", "w3"):
+            deal_words(m, 0)
+            deal_scales(m)
         first_layer(*blocks[0])
         deal_words("w2", 0)
         deal_scales("w2")
-        for step in range(count + 1):
-            if step + 2 < count:
-                gather(*blocks[step + 2])
-            if step < count:
-                quantise_hidden(*blocks[step])
-            if step + 1 < count:
+        for step in range(len(blocks)):
+            if step + 2 < len(blocks):
+                gather_for(*blocks[step + 2])
+            quantise_hidden(*blocks[step])
+            if step + 1 < len(blocks):
                 first_layer(*blocks[step + 1])
-            if step < held_back:
+            if step < before_last_expert:
                 second_layer(*blocks[step])
-            nxt = step // BLOCKS + 1
-            if nxt < E:
-                if step % BLOCKS == 0:
-                    deal_words("w1", nxt)
-                    deal_words("w3", nxt)
-                if step % BLOCKS == 1:
-                    deal_words("w2", nxt)
-            if 0 <= step - 1 < held_back:
-                for d in range(PACK):
-                    scatter(*blocks[step - 1], d)
-        order = [0, 3, 1, 2]
-        e = E - 1
-        for j, d in enumerate(order):
-            res = psum.tile([P, SLOTS], F32, name="res" if j < 3 else "lin", bufs=3)
-            gated = keep.tile([P, SLOTS], F32, name=f"gated_last_{d}")
-            for cols in (slice(0, C), slice(C, SLOTS)):
-                product(res[:, cols], "w2", e, d, hid_words[e][:, cols], hid_scales[e][:, cols])
-            nc.vector.tensor_tensor(out=gated[:], in0=res[:], in1=gates[e][:], op=MULT)
-            results[d] = gated
-        def scatter_last(d):
-            first_window = first_win[d][:].indirect(first_list[:, e * C // LIST_COL :])
-            second_window = second_win[d][:].indirect(second_offsets(e))
-            for part, (window, cols) in enumerate(((first_window, slice(0, C)), (second_window, slice(C, SLOTS)))):
-                if d == 3:
-                    nc.vector.tensor_copy(window, results[d][:, cols])
-                else:
-                    nc.scalar.activation(out=window, in_=results[d][:, cols], func=COPY)
+            e, b = blocks[step]
+            if e + 1 < E and b == 0:
+                deal_words("w1", e + 1)
+                deal_words("w3", e + 1)
+            if e + 1 < E and b == 1:
+                deal_words("w2", e + 1)
+            if 1 <= step <= before_last_expert:
+                scatter_block(*blocks[step - 1])
 
-        for d in order:
-            scatter_last(d)
-        for d in [3, 0, 1]:
-            finish(d, slice(0, T))
+        last = E - 1
+        scalar_row_sets = [d for d in range(PACK) if d != VECTOR_ROW_SET]
+        row_sets = scalar_row_sets[:1] + [VECTOR_ROW_SET] + scalar_row_sets[1:]
+        first_cols, second_cols = slice(0, C), slice(C, SLOTS)
+        gated_rows = {}
+        for d in row_sets:
+            res = psum.tile([P, SLOTS], F32, name="lin" if d == row_sets[-1] else "res", bufs=3)
+            gated = keep.tile([P, SLOTS], F32, name=f"gated_last_{d}")
+            for cols in (first_cols, second_cols):
+                product(res[:, cols], "w2", last, d, hid_words[last][:, cols], hid_scales[last][:, cols])
+            nc.vector.tensor_tensor(out=gated[:], in0=res[:], in1=gates[last][:], op=MULT)
+            gated_rows[d] = gated
+        for d in row_sets:
+            scatter(d, first_win[d], first_offsets(last * C, C), gated_rows[d][:, first_cols])
+            scatter(d, second_win[d], second_offsets(last), gated_rows[d][:, second_cols])
+        for d in [VECTOR_ROW_SET] + scalar_row_sets[:-1]:
+            add_choices(d, slice(0, T))
             nc.sync.dma_start(out=out_rows[:, d, :], in_=total[:, d, :])
 
-        last = order[-1]
+        final_set = row_sets[-1]
         chunks = [slice(c * CHUNK, (c + 1) * CHUNK) for c in range(T // CHUNK)]
         for cols in chunks:
-            finish(last, cols)
-        nc.sync.dma_start(out=out_rows[:, last, :], in_=total[:, last, :])
-        words_out = out_1[0].rearrange("p t d -> p (t d)").bitcast(I32)
+            add_choices(final_set, cols)
+        nc.sync.dma_start(out=out_rows[:, final_set, :], in_=total[:, final_set, :])
         for c, cols in enumerate(chunks):
-            dst = total_bf[:, cols, :].rearrange("p (c i) d -> p c d i", i=4)
-            src = total[:, :, cols].rearrange("p d (c i) -> p c d i", i=4)
+            dst = total_bf[:, cols, :].rearrange("p (g i) d -> p g d i", i=4)
+            src = total[:, :, cols].rearrange("p d (g i) -> p g d i", i=4)
             if c % 2 == 0:
                 nc.scalar.copy(out=dst, in_=src)
             else:
                 nc.vector.tensor_copy(out=dst, in_=src)
-        for c in (1, 0, 3, 2):
-            cols = chunks[c]
-            nc.vector.quantize_mx(
-                out=out_words[:, cols].bitcast(FP8X4),
-                scales=out_scales[:, cols],
-                in_=total_bf[:, cols, :].rearrange("p t d -> p (t d)"),
-            )
-            nc.sync.dma_start(out=words_out[:, cols], in_=out_words[:, cols].bitcast(I32))
+        words_out = out_1[0].rearrange("p t d -> p (t d)").bitcast(I32)
+        for pair in range(0, len(chunks), 2):
+            for cols in (chunks[pair + 1], chunks[pair]):
+                nc.vector.quantize_mx(
+                    out=out_words[:, cols].bitcast(FP8X4),
+                    scales=out_scales[:, cols],
+                    in_=total_bf[:, cols, :].rearrange("p t d -> p (t d)"),
+                )
+                nc.sync.dma_start(out=words_out[:, cols], in_=out_words[:, cols].bitcast(I32))
         for q in range(QUADS):
             queue = nc.sync if q % 2 == 0 else nc.scalar
             queue.dma_start(

from contextlib import ExitStack

import concourse.mybir as mybir

K, T, E, C, D, H, N = 512, 1024, 4, 256, 128, 512, 512
FLOPS = 2 * E * (C + D) * (2 * K * H + H * N)

F32 = mybir.dt.float32
BF16 = mybir.dt.bfloat16
I32 = mybir.dt.int32
U32 = mybir.dt.uint32
U16 = mybir.dt.uint16
U8 = mybir.dt.uint8
FP8X4 = mybir.dt.float8_e4m3fn_x4
MULT = mybir.AluOpType.mult
ADD = mybir.AluOpType.add
SILU = mybir.ActivationFunctionType.Silu
COPY = mybir.ActivationFunctionType.Copy

P = 128
PACK = 4
QUADS = 4
LIST_COL = 16
BLOCK = 128
SLOTS = C + D
BLOCKS = SLOTS // BLOCK
FIRST_BLOCKS = C // BLOCK
VECTOR_ROW_SET = 3
CHUNK = 256


def tile_moe_ada_glu_silu_kernel(
    tc, x_words, x_scales, w1_words, w1_scales, w3_words, w3_scales, w2_words, w2_scales,
    gate1, gate2, offs, offs2, out_0, out_1, out_2,
):
    nc = tc.nc
    with ExitStack() as ctx:
        keep = ctx.enter_context(tc.tile_pool(name="keep", bufs=1))
        psum = ctx.enter_context(tc.psum_pool(name="psum", bufs=1))

        def held(shape, dtype, name):
            return keep.tile(shape, dtype, name=name, align_bytes=64)

        first_list = keep.tile([P, E * C // LIST_COL], U16, name="first_list")
        second_list = keep.tile([P, E * D // LIST_COL], U16, name="second_list")
        tok_words = held([P, T], U32, "tok_words")
        tok_scales = held([P, T], U8, "tok_scales")
        words_in = {"w1": w1_words, "w3": w3_words, "w2": w2_words}
        scales_in = {"w1": w1_scales, "w3": w3_scales, "w2": w2_scales}
        raw_words = {(m, e): held([P, H], U32, f"raw_{m}_{e}") for m in words_in for e in range(E)}
        dealt_words = {(m, e): held([P, H], U32, f"dealt_{m}_{e}") for m in words_in for e in range(E)}
        raw_scales = {m: held([P, H], U8, f"raw_scales_{m}") for m in words_in}
        dealt_scales = {m: held([P, H], U8, f"dealt_scales_{m}") for m in words_in}
        gates = [held([P, SLOTS], F32, f"gates_{e}") for e in range(E)]
        hidden = [held([P, SLOTS, PACK], BF16, f"hidden_{e}") for e in range(E)]
        hid_words = [held([P, SLOTS], U32, f"hid_words_{e}") for e in range(E)]
        hid_scales = [held([P, SLOTS], U8, f"hid_scales_{e}") for e in range(E)]
        first_win = [held([P, T], F32, f"first_win_{d}") for d in range(PACK)]
        second_win = [held([P, T], F32, f"second_win_{d}") for d in range(PACK)]
        total = held([P, PACK, T], F32, "total")
        total_bf = held([P, T, PACK], BF16, "total_bf")
        out_words = held([P, T], U32, "out_words")
        out_scales = held([P, T], U8, "out_scales")

        nc.gpsimd.memset(tok_scales[:].bitcast(I32), 0)
        for m in raw_scales:
            nc.gpsimd.memset(raw_scales[m][:].bitcast(I32), 0)
        for d in range(PACK):
            engine = nc.vector if d < PACK // 2 else nc.gpsimd
            engine.memset(second_win[d][:], 0.0)

        def load_weight_scales(m, quads):
            for q in quads:
                nc.sync.dma_start(
                    out=raw_scales[m][32 * q : 32 * q + 4 * E, :].bitcast(I32),
                    in_=scales_in[m][:, 0, 4 * q : 4 * q + 4, :].bitcast(I32),
                )

        def load_weight_words(m, e):
            nc.sync.dma_start(
                out=raw_words[m, e][:].bitcast(I32),
                in_=words_in[m][e, 0].rearrange("p n d -> p (n d)").bitcast(I32),
            )

        def load_first_gate(e):
            nc.sync.dma_start(out=gates[e][:, 0:C], in_=gate1[:, e * C : (e + 1) * C])

        def load_second_gate(e):
            nc.sync.dma_start(out=gates[e][:, C:SLOTS], in_=gate2[:, e * D : (e + 1) * D])

        nc.sync.dma_start(first_list[:], offs)
        for q in range(QUADS):
            nc.sync.dma_start(
                out=tok_scales[32 * q : 32 * q + 4, :].bitcast(I32),
                in_=x_scales[0, 4 * q : 4 * q + 4, :].bitcast(I32),
            )
        load_weight_scales("w1", range(0, QUADS // 2))
        nc.sync.dma_start(
            out=tok_words[:].bitcast(I32), in_=x_words[0].rearrange("p t d -> p (t d)").bitcast(I32)
        )
        load_weight_words("w1", 0)
        load_weight_scales("w1", range(QUADS // 2, QUADS))
        load_weight_words("w3", 0)
        load_weight_scales("w3", range(QUADS))
        nc.sync.dma_start(second_list[:], offs2)
        load_weight_scales("w2", range(QUADS))
        for e in range(E - 1):
            load_weight_words("w1", e + 1)
            load_weight_words("w2", e)
            load_first_gate(e)
            load_weight_words("w3", e + 1)
            load_second_gate(e)
        load_weight_words("w2", E - 1)
        load_first_gate(E - 1)
        load_second_gate(E - 1)

        def first_offsets(start, width):
            return first_list[:, start // LIST_COL : (start + width) // LIST_COL]

        def second_offsets(e):
            return second_list[:, e * D // LIST_COL : (e + 1) * D // LIST_COL]

        slots = {}

        def gather(name, offsets, e, first_block, width):
            words = held([P, width], U32, f"{name}_words")
            scales = held([P, width], U8, f"{name}_scales")
            nc.vector.tensor_copy(scales[:], tok_scales[:].indirect(offsets))
            nc.vector.tensor_copy(words[:], tok_words[:].indirect(offsets))
            for j in range(width // BLOCK):
                part = slice(j * BLOCK, (j + 1) * BLOCK)
                slots[e, first_block + j] = (words[:, part], scales[:, part])

        def gather_for(e, b):
            if b == 0:
                gather("first_slot", first_offsets(e * C, C), e, b, C)
            if b == FIRST_BLOCKS:
                gather("second_slot", second_offsets(e), e, b, D)

        dealt_by_scalar = [("w2", 0), ("w1", 1), ("w3", 1)]

        def deal_words(m, e):
            dst = dealt_words[m, e][:].rearrange("p (d r) -> p r d", d=PACK)
            src = raw_words[m, e][:].rearrange("p (r d) -> p r d", d=PACK)
            if (m, e) in dealt_by_scalar:
                nc.scalar.copy(out=dst, in_=src)
            else:
                nc.vector.tensor_copy(out=dst.bitcast(I32), in_=src.bitcast(I32))

        def deal_scales(m):
            nc.vector.tensor_copy(
                out=dealt_scales[m][:].rearrange("p (d r) -> p d r", d=PACK),
                in_=raw_scales[m][:].rearrange("p (r d) -> p d r", d=PACK),
            )

        def product(out, m, e, d, words, scales):
            cols = slice(d * P, (d + 1) * P)
            nc.tensor.matmul_mx(
                out=out,
                lhsT=dealt_words[m, e][:, cols].bitcast(FP8X4),
                lhsT_scale=dealt_scales[m][4 * e : P, cols],
                rhs=words.bitcast(FP8X4),
                rhs_scale=scales,
                start=True,
                stop=True,
            )

        def block_cols(b):
            return slice(b * BLOCK, (b + 1) * BLOCK)

        def first_layer(e, b):
            pre = psum.tile([P, PACK, BLOCK], F32, name="pre", bufs=2)
            lin = psum.tile([P, PACK, BLOCK], F32, name="lin", bufs=3)
            for bank, m in ((pre, "w1"), (lin, "w3")):
                for d in range(PACK):
                    product(bank[:, d, :], m, e, d, *slots[e, b])
            act = keep.tile([P, BLOCK, PACK], F32, name="act", bufs=2)
            nc.scalar.activation(out=act[:], in_=pre[:].rearrange("p d s -> p s d"), func=SILU)
            nc.vector.tensor_tensor(
                out=hidden[e][:, block_cols(b), :], in0=lin[:].rearrange("p d s -> p s d"), in1=act[:], op=MULT
            )

        def quantise_hidden(e, b):
            cols = block_cols(b)
            nc.vector.quantize_mx(
                out=hid_words[e][:, cols].bitcast(FP8X4),
                scales=hid_scales[e][:, cols],
                in_=hidden[e][:, cols, :].rearrange("p s d -> p (s d)"),
            )

        gated_blocks = {}

        def second_layer(e, b):
            cols = block_cols(b)
            res = psum.tile([P, PACK, BLOCK], F32, name="res", bufs=3)
            for d in range(PACK):
                product(res[:, d, :], "w2", e, d, hid_words[e][:, cols], hid_scales[e][:, cols])
            gated = keep.tile([P, PACK, BLOCK], F32, name=f"gated_{e}_{b}")
            gate = gates[e][:, cols].unsqueeze(1).broadcast_to([P, PACK, BLOCK])
            nc.vector.tensor_tensor(out=gated[:], in0=res[:], in1=gate, op=MULT)
            gated_blocks[e, b] = gated

        def scatter(d, window, offsets, values):
            if d == VECTOR_ROW_SET:
                nc.vector.tensor_copy(window[:].indirect(offsets), values)
            else:
                nc.scalar.activation(out=window[:].indirect(offsets), in_=values, func=COPY)

        def scatter_block(e, b):
            for d in range(PACK):
                values = gated_blocks[e, b][:, d, :]
                if b < FIRST_BLOCKS:
                    scatter(d, first_win[d], first_offsets(e * C + b * BLOCK, BLOCK), values)
                else:
                    scatter(d, second_win[d], second_offsets(e), values)

        def add_choices(d, cols):
            nc.vector.tensor_tensor(
                out=total[:, d, cols], in0=first_win[d][:, cols], in1=second_win[d][:, cols], op=ADD
            )

        out_rows = out_0.rearrange("(p d) t -> p d t", d=PACK)

        blocks = [(e, b) for e in range(E) for b in range(BLOCKS)]
        before_last_expert = len(blocks) - BLOCKS
        gather_for(*blocks[0])
        for m in ("w1", "w3"):
            deal_words(m, 0)
            deal_scales(m)
        first_layer(*blocks[0])
        deal_words("w2", 0)
        deal_scales("w2")
        for step in range(len(blocks)):
            if step + 2 < len(blocks):
                gather_for(*blocks[step + 2])
            quantise_hidden(*blocks[step])
            if step + 1 < len(blocks):
                first_layer(*blocks[step + 1])
            if step < before_last_expert:
                second_layer(*blocks[step])
            e, b = blocks[step]
            if e + 1 < E and b == 0:
                deal_words("w1", e + 1)
                deal_words("w3", e + 1)
            if e + 1 < E and b == 1:
                deal_words("w2", e + 1)
            if 1 <= step <= before_last_expert:
                scatter_block(*blocks[step - 1])

        last = E - 1
        scalar_row_sets = [d for d in range(PACK) if d != VECTOR_ROW_SET]
        row_sets = scalar_row_sets[:1] + [VECTOR_ROW_SET] + scalar_row_sets[1:]
        first_cols, second_cols = slice(0, C), slice(C, SLOTS)
        gated_rows = {}
        for d in row_sets:
            res = psum.tile([P, SLOTS], F32, name="lin" if d == row_sets[-1] else "res", bufs=3)
            gated = keep.tile([P, SLOTS], F32, name=f"gated_last_{d}")
            for cols in (first_cols, second_cols):
                product(res[:, cols], "w2", last, d, hid_words[last][:, cols], hid_scales[last][:, cols])
            nc.vector.tensor_tensor(out=gated[:], in0=res[:], in1=gates[last][:], op=MULT)
            gated_rows[d] = gated
        for d in row_sets:
            scatter(d, first_win[d], first_offsets(last * C, C), gated_rows[d][:, first_cols])
            scatter(d, second_win[d], second_offsets(last), gated_rows[d][:, second_cols])
        for d in [VECTOR_ROW_SET] + scalar_row_sets[:-1]:
            add_choices(d, slice(0, T))
            nc.sync.dma_start(out=out_rows[:, d, :], in_=total[:, d, :])

        final_set = row_sets[-1]
        chunks = [slice(c * CHUNK, (c + 1) * CHUNK) for c in range(T // CHUNK)]
        for cols in chunks:
            add_choices(final_set, cols)
        nc.sync.dma_start(out=out_rows[:, final_set, :], in_=total[:, final_set, :])
        for c, cols in enumerate(chunks):
            dst = total_bf[:, cols, :].rearrange("p (g i) d -> p g d i", i=4)
            src = total[:, :, cols].rearrange("p d (g i) -> p g d i", i=4)
            if c % 2 == 0:
                nc.scalar.copy(out=dst, in_=src)
            else:
                nc.vector.tensor_copy(out=dst, in_=src)
        words_out = out_1[0].rearrange("p t d -> p (t d)").bitcast(I32)
        for pair in range(0, len(chunks), 2):
            for cols in (chunks[pair + 1], chunks[pair]):
                nc.vector.quantize_mx(
                    out=out_words[:, cols].bitcast(FP8X4),
                    scales=out_scales[:, cols],
                    in_=total_bf[:, cols, :].rearrange("p t d -> p (t d)"),
                )
                nc.sync.dma_start(out=words_out[:, cols], in_=out_words[:, cols].bitcast(I32))
        for q in range(QUADS):
            queue = nc.sync if q % 2 == 0 else nc.scalar
            queue.dma_start(
                out=out_2[0, 4 * q : 4 * q + 4, :].bitcast(I32),
                in_=out_scales[32 * q : 32 * q + 4, :].bitcast(I32),
            )
